import numpy as np
import ml_dtypes


def mxq(x, axis, fmt="e4m3"):
    dtype, down = {"e4m3": (ml_dtypes.float8_e4m3fn, 7), "e5m2": (ml_dtypes.float8_e5m2, 14)}[fmt]
    v = np.moveaxis(np.asarray(x, np.float32).astype(ml_dtypes.bfloat16).astype(np.float64), axis, -1)
    blocks = v.reshape(v.shape[:-1] + (-1, 32))
    amax = np.abs(blocks).max(-1, keepdims=True)
    byte = np.maximum(np.where(amax > 0, np.frexp(amax)[1] - 1 + 127, 0) - down, 1)
    scale = np.exp2(byte - 127.0)
    codes = (blocks / scale).astype(np.float32).astype(dtype).astype(np.float64)
    return np.moveaxis((codes * scale).reshape(v.shape), -1, axis)


WIDE = False


def mx_kscale(k):
    if not WIDE:
        return np.ones(k)
    levels = np.array([10, -10, 5, -5, 0])
    if k % 512:
        return np.exp2(np.random.permutation(np.resize(levels, k // 32))).repeat(32)
    a = np.empty((k // 512, 16))
    for p in range(k // 512):
        a[p, :8] = np.random.permutation(np.resize(levels, 8))
        for g in range(8):
            far = levels[np.abs(levels - a[p, g]) >= 10]
            a[p, g + 8] = far[np.random.randint(len(far))]
    return np.exp2(a.ravel()).repeat(32)


BF16 = ml_dtypes.bfloat16


def bf(x):
    return np.asarray(x, np.float32).astype(BF16)


def f64(x):
    return np.asarray(x).astype(np.float64)


E2M1 = np.array([0.0, 0.5, 1.0, 1.5, 2.0, 3.0, 4.0, 6.0, -0.0, -0.5, -1.0, -1.5, -2.0, -3.0, -4.0, -6.0])


def pack_weight(w, fmt):
    k, n = w.shape
    w = f64(bf(w)).reshape(k // 32, 32, n)
    amax = np.abs(w).max(1)
    if fmt == "e4m3":
        byte = np.frexp(amax)[1] - 1 + 127 - 7
    else:
        mant, ex = np.frexp(amax / 6.0)
        byte = np.where(mant > 0.5, ex, ex - 1) + 127
    byte = np.clip(np.where(amax > 0, byte, 1), 1, 254)
    scaled = (w * np.exp2(127.0 - byte)[:, None, :]).reshape(k, n).astype(np.float32)
    by_word = np.ascontiguousarray(scaled.reshape(k // 512, 128, 4, n).transpose(0, 1, 3, 2))
    if fmt == "e4m3":
        words = by_word.astype(ml_dtypes.float8_e4m3fn).view(np.uint8)
    else:
        c = by_word.astype(ml_dtypes.float4_e2m1fn).view(np.uint8) & 0xF
        words = c[..., 0::2] | (c[..., 1::2] << 4)
    return np.ascontiguousarray(words), np.ascontiguousarray(byte.astype(np.uint8).reshape(k // 512, 16, n))


def unpack_weight(words, scales, fmt):
    g, p, n, _ = words.shape
    if fmt == "e4m3":
        vals = np.ascontiguousarray(words).view(ml_dtypes.float8_e4m3fn).astype(np.float64)
    else:
        nib = np.empty((g, p, n, 4), np.uint8)
        nib[..., 0::2] = words & 0xF
        nib[..., 1::2] = words >> 4
        vals = E2M1[nib]
    vals = vals * np.repeat(np.exp2(scales.astype(np.float64) - 127.0), 8, axis=1)[..., None]
    return vals.transpose(0, 1, 3, 2).reshape(g * 512, n)
def pack4(w):
    words, scales = pack_weight(w, "e2m1")
    return words.reshape(words.shape[0], 128, -1), scales


def unpack4(words, scales):
    return unpack_weight(words.reshape(words.shape[0], 128, -1, 2), scales, "e2m1")


D, P, B = 2048, 1024, 512


def draw0():
    s, t = mx_kscale(P), mx_kscale(D)
    pattern = np.random.standard_normal((D, P))
    decode = (pattern + np.random.standard_normal((D, P))) / np.sqrt(2 * D)
    dec_words, dec_scales = pack4(decode / t[:, None])
    noise = np.exp(0.3 * np.random.standard_normal((D, B)))
    return {"mask": bf(pattern / np.sqrt(P) * s),
            "scenes": bf(np.random.standard_normal((B, P)) / s),
            "dark": bf(0.3 * np.random.standard_normal(D)),
            "inv_sigma": bf(noise * t[:, None]),
            "dec_words": dec_words,
            "dec_scales": dec_scales}


def core(mask, scenes, dark, inv_sigma, dec_words, dec_scales):
    a = mxq(f64(mask), 1, "e4m3")
    x = mxq(f64(scenes), 1, "e4m3")
    y = a @ x.T
    z = (y - f64(dark)[:, None]) * f64(inv_sigma)
    g = unpack4(dec_words, dec_scales)
    image = g.T @ mxq(z, 0, "e4m3")
    return image


def e4m3fn_bytes(y):
    return np.clip(np.asarray(y, np.float64), -448.0, 448.0).astype(np.float32).astype(ml_dtypes.float8_e4m3fn).view(np.uint8)


def e4m3fn_values(b):
    return np.asarray(b, np.uint8).view(ml_dtypes.float8_e4m3fn).astype(np.float64)


def setup_inputs():
    d = draw0()
    x0 = np.asarray(d['mask']).astype(np.float64)
    s = (np.max(np.abs(x0), axis=(0,), keepdims=True) / 448.0).astype(np.float32)
    out = {}
    for k, v in d.items():
        if k == 'mask':
            out['mask_bytes'] = e4m3fn_bytes(x0 / s.astype(np.float64))
            out['mask_scale'] = s
        else:
            out[k] = v
    return out


def reference(mask_bytes, mask_scale, scenes, dark, inv_sigma, dec_words, dec_scales):
    return core(e4m3fn_values(mask_bytes) * mask_scale.astype(np.float64), scenes, dark, inv_sigma, dec_words, dec_scales)

@@ -1,0 +1,391 @@
+import concourse.mybir as mybir
+from concourse.masks import make_identity
+from contextlib import ExitStack
+
+F32 = mybir.dt.float32
+BF16 = mybir.dt.bfloat16
+U32 = mybir.dt.uint32
+I32 = mybir.dt.int32
+U8 = mybir.dt.uint8
+FP8 = mybir.dt.float8_e4m3fn
+E4M3X4 = mybir.dt.float8_e4m3fn_x4
+E2M1X4 = mybir.dt.float4_e2m1fn_x4
+ALU = mybir.AluOpType
+
+D, P, B = 2048, 1024, 512
+QZ_STEP = [3, 6, 8]
+QZ_FIRST = [0, 1, 1]
+FLOPS = 2 * 2 * D * P * B
+
+NP = 128
+NG = D // 512
+NPAIR = 2 * NG
+NC = P // 512
+NM = P // 128
+FORM = [("B", 512, 0), ("A", 512), ("A", 512), ("B", 0, 192)]
+W_FIRST = True
+G_PIECE = 128
+MID_STEP = 0
+
+
+def tile_coded_aperture_backprojection_s13_kernel(
+    tc, mask_bytes, mask_scale, scenes, dark, inv_sigma, dec_words, dec_scales, out
+):
+    nc = tc.nc
+    with ExitStack() as ctx:
+        keep = ctx.enter_context(tc.tile_pool(name="keep", bufs=1))
+        work = ctx.enter_context(tc.tile_pool(name="work", bufs=2))
+        psum = ctx.enter_context(tc.psum_pool(name="psum", bufs=1))
+        ctx.enter_context(tc.manual_schedule())
+
+        dummy = keep.tile([NP, 2], F32, name="dummy")
+        nc.vector.memset(dummy[:], 0.0)
+        nc.scalar.copy(out=dummy[:, 1:2], in_=dummy[:, 0:1])
+
+        mscale = keep.tile([NP, NC, 2, 2], F32, name="mscale")
+        nc.scalar.dma_start(
+            out=mscale[:], in_=mask_scale.rearrange("o (c p u e) -> p (o c) u e", c=NC, p=NP, u=2, e=2)
+        )
+        ident = keep.tile([NP, NP], F32, name="ident")
+        make_identity(nc, ident[:])
+        gsc = keep.tile([NP, NG, P], U8, name="gsc", align_bytes=64)
+        nc.gpsimd.memset(gsc[:].bitcast(I32), 0)
+        darks = keep.tile([NP, NG, 4], BF16, name="darks")
+        nc.gpsimd.dma_start(out=darks[:], in_=dark.rearrange("(g p t) -> p g t", g=NG, p=NP, t=4))
+
+        negd = keep.tile([NP, NG, 4], F32, name="negd")
+        nc.gpsimd.tensor_scalar(out=negd[:], in0=darks[:], scalar1=-1.0, scalar2=None, op0=ALU.mult)
+
+        mask_v = mask_bytes.rearrange("(g p t) k -> g p t k", g=NG, p=NP, t=4)
+        sig_v = inv_sigma.rearrange("(g p t) b -> g p t b", g=NG, p=NP, t=4)
+        scn_v = scenes.rearrange("(r p) k -> r p k", p=NP)
+
+        mb = [keep.tile([NP, 2, P], U8, name=f"mb{j}", align_bytes=64) for j in range(NPAIR)]
+        sig = [keep.tile([NP, 4, B], BF16, name=f"sig{g}", align_bytes=64) for g in range(NG)]
+        scn = [keep.tile([NP, P], BF16, name=f"scn{r}", align_bytes=64) for r in range(4)]
+        gw = [keep.tile([NP, 2 * P], U8, name=f"gw{g}", align_bytes=64) for g in range(NG)]
+
+        def load_mask(j):
+            g, h = divmod(j, 2)
+            nc.sync.dma_start(out=mb[j][:], in_=mask_v[g][:, 2 * h : 2 * h + 2, :])
+
+        for j in range(2):
+            for t in range(2):
+                nc.sync.dma_start(out=mb[j][:, t, :], in_=mask_v[0][:, 2 * j + t, :])
+        for r in range(4):
+            nc.sync.dma_start(out=scn[r][:], in_=scn_v[r])
+        load_mask(2)
+        nc.sync.dma_start(out=sig[0][:], in_=sig_v[0])
+        for j in range(3, 8):
+            load_mask(j)
+            if j % 2 == 0:
+                nc.sync.dma_start(out=sig[j // 2 - 1][:], in_=sig_v[j // 2 - 1])
+        nc.sync.dma_start(out=sig[3][:], in_=sig_v[3])
+        for q in range(4):
+            nc.sync.dma_start(
+                out=gsc[32 * q : 32 * q + 4].bitcast(I32),
+                in_=dec_scales[:, 4 * q : 4 * q + 4, :].bitcast(I32).rearrange("g q n -> q g n"),
+            )
+        for g in range(NG):
+            nc.sync.dma_start(out=gw[g][:].bitcast(I32), in_=dec_words[g].bitcast(I32))
+
+        scodes = keep.tile([NP, NC, B], U32, name="scodes", align_bytes=64)
+        sscales = keep.tile([NP, NC, B], U8, name="sscales", align_bytes=64)
+        zcodes = [keep.tile([NP, B], U32, name=f"zcodes{g}", align_bytes=64) for g in range(NG)]
+        zscales = [keep.tile([NP, B], U8, name=f"zscales{g}", align_bytes=64) for g in range(NG)]
+
+        wide = {}
+        tbank = {}
+        qin = {}
+        codes = {}
+        scales = {}
+        ybank = {}
+        zt = {}
+        ysb = {}
+        zq = {}
+        img = {}
+        part = {}
+
+        def bank(tag, shape, name):
+            t = psum.tile(shape, F32, name=name, tag=tag)
+            return t
+
+        def widen(j, t, engine):
+            if t == 0:
+                wide[j] = work.tile([NP, 2, P], BF16, name=f"wide{j}", tag="wide", bufs=3, align_bytes=64)
+            src = mb[j][:, t, :].bitcast(FP8)
+            if engine == "v":
+                nc.vector.tensor_copy(out=wide[j][:, t, :], in_=src)
+            else:
+                nc.scalar.copy(out=wide[j][:, t, :], in_=src)
+
+        def widen_pair(j):
+            wide[j] = work.tile([NP, 2, P], BF16, name=f"wide{j}", tag="wide", bufs=3, align_bytes=64)
+            nc.scalar.copy(
+                out=wide[j][:].rearrange("p t k -> p (t k)"), in_=mb[j][:].rearrange("p t k -> p (t k)").bitcast(FP8)
+            )
+
+        def turn(tiles, c, tag, name):
+            bk = bank(tag, [NP, 2, 256], name)
+            for t in range(2):
+                for u in range(2):
+                    nc.tensor.transpose(
+                        bk[:, u, 128 * t : 128 * t + 128], tiles[t][:, 256 * c + u : 256 * (c + 1) : 2], ident[:]
+                    )
+            return bk
+
+        def turn_mask(j, c):
+            w = wide[j][:].bitcast(F32)
+            tbank[j, c] = turn([w[:, 0, :], w[:, 1, :]], c, f"t{c}", f"tb{j}_{c}")
+
+        def scale_mask(j, c):
+            if c == 0:
+                qin[j] = work.tile([NP, NC, 256, 4], BF16, name=f"qin{j}", tag="qin", bufs=2, align_bytes=64)
+            nc.vector.tensor_tensor(
+                out=qin[j][:, c].rearrange("p x (u e) -> p x u e", u=2),
+                in0=tbank[j, c][:].bitcast(BF16).rearrange("p u (x e) -> p x u e", e=2),
+                in1=mscale[:, c : c + 1].to_broadcast([NP, 256, 2, 2]),
+                op=ALU.mult,
+            )
+
+        def quant_mask(j):
+            codes[j] = work.tile([NP, NC, 256], U32, name=f"codes{j}", tag="codes", bufs=3, align_bytes=64)
+            scales[j] = work.tile([NP, NC, 256], U8, name=f"scales{j}", tag="scales", bufs=3, align_bytes=64)
+            nc.vector.quantize_mx(
+                out=codes[j][:].rearrange("p c x -> p (c x)").bitcast(E4M3X4),
+                scales=scales[j][:].rearrange("p c x -> p (c x)"),
+                in_=qin[j][:].rearrange("p c x t -> p (c x t)"),
+            )
+
+        def project(j, t):
+            ybank[j, t] = bank(f"y{t}", [NP, B], f"y{j}_{t}")
+            cols = slice(128 * t, 128 * t + 128)
+            for c in range(NC):
+                nc.tensor.matmul_mx(
+                    out=ybank[j, t][:],
+                    lhsT=codes[j][:, c, cols].bitcast(E4M3X4),
+                    lhsT_scale=scales[j][:, c, cols],
+                    rhs=scodes[:, c, :].bitcast(E4M3X4),
+                    rhs_scale=sscales[:, c, :],
+                    start=(c == 0),
+                    stop=(c == NC - 1),
+                )
+
+        def whiten(j, t):
+            g, h = divmod(j, 2)
+            s = 2 * h + t
+            if s == 0:
+                zt[g] = work.tile([NP, 4, B], BF16, name=f"zt{g}", tag="zt", bufs=2, align_bytes=64)
+            nc.vector.scalar_tensor_tensor(
+                out=zt[g][:, s, :],
+                in0=ybank[j, t][:],
+                scalar=darks[:, g, s : s + 1],
+                in1=sig[g][:, s, :],
+                op0=ALU.subtract,
+                op1=ALU.mult,
+            )
+
+        def subtract_dark(j, t):
+            g, h = divmod(j, 2)
+            s = 2 * h + t
+            if s == 0:
+                ysb[g] = work.tile([NP, 4, B], F32, name=f"ysb{g}", tag="ysb", bufs=2, align_bytes=64)
+            nc.scalar.activation(
+                out=ysb[g][:, s, :],
+                in_=ybank[j, t][:],
+                func=mybir.ActivationFunctionType.Identity,
+                bias=negd[:, g, s : s + 1],
+                scale=1.0,
+            )
+
+        def weigh(g, b0, b1, engine):
+            if b0 == 0:
+                zq[g] = work.tile([NP, B, 4], BF16, name=f"zq{g}", tag="zq", bufs=2, align_bytes=64)
+            engine.tensor_tensor(
+                out=zq[g][:, b0:b1, :],
+                in0=ysb[g][:, :, b0:b1].rearrange("p t b -> p b t"),
+                in1=sig[g][:, :, b0:b1].rearrange("p t b -> p b t"),
+                op=ALU.mult,
+            )
+
+        def interleave(g, b0, b1, engine):
+            if b0 == 0:
+                zq[g] = work.tile([NP, B, 4], BF16, name=f"zq{g}", tag="zq", bufs=2, align_bytes=64)
+            dst = zq[g][:, b0:b1, :]
+            src = zt[g][:, :, b0:b1].rearrange("p t b -> p b t")
+            if engine == "v":
+                nc.vector.tensor_copy(out=dst, in_=src)
+            elif engine == "g":
+                nc.gpsimd.tensor_scalar(out=dst, in0=src, scalar1=1.0, scalar2=0.0, op0=ALU.mult, op1=ALU.add)
+            else:
+                nc.scalar.copy(out=dst, in_=src)
+
+        def finish_z(g):
+            form = FORM[g]
+            if form[0] == "A":
+                for b0 in range(0, form[1], G_PIECE):
+                    weigh(g, b0, b0 + G_PIECE, nc.gpsimd)
+                if form[1] < B:
+                    weigh(g, form[1], B, nc.vector)
+            else:
+                b0 = 0
+                while b0 < form[1]:
+                    interleave(g, b0, b0 + 128, "g")
+                    b0 += 128
+                if form[2]:
+                    n = 1 if form[2] <= 256 else 2
+                    for i in range(n):
+                        interleave(g, b0, b0 + form[2] // n, "s")
+                        b0 += form[2] // n
+                if b0 < B:
+                    interleave(g, b0, B, "v")
+
+        def quant_z(g, b0, b1):
+            nc.vector.quantize_mx(
+                out=zcodes[g][:, b0:b1].bitcast(E4M3X4),
+                scales=zscales[g][:, b0:b1],
+                in_=zq[g][:, b0:b1, :].rearrange("p b t -> p (b t)"),
+            )
+
+        IMG_TAG = ["m0", "m1", "m2", "m3", "t0", "t1", "y0", "y1"]
+        LAST = NG - 1
+
+        def image_pass(bk, m, g, start, stop):
+            nc.tensor.matmul_mx(
+                out=bk[:],
+                lhsT=gw[g][:, 256 * m : 256 * (m + 1)].bitcast(E2M1X4),
+                lhsT_scale=gsc[:, g, 128 * m : 128 * (m + 1)],
+                rhs=zcodes[g][:].bitcast(E4M3X4),
+                rhs_scale=zscales[g][:],
+                start=start,
+                stop=stop,
+            )
+
+        pbank = {}
+
+        def early(g):
+            for m in range(4, NM):
+                if g == 0:
+                    pbank[m] = bank(f"m{m - 4}", [NP, B], f"early{m}")
+                image_pass(pbank[m], m, g, g == 0, g == 1)
+
+        def park():
+            for m in range(4, NM):
+                part[m] = keep.tile([NP, B], F32, name=f"part{m}")
+                nc.scalar.copy(out=part[m][:], in_=pbank[m][:])
+
+        def backproject(m, g):
+            first = 0 if m < 4 else 2
+            if g == first:
+                img[m] = bank(IMG_TAG[m], [NP, B], f"img{m}")
+            image_pass(img[m], m, g, g == first, g == LAST)
+
+        def widen_part(j, t, c, engine):
+            cols = slice(512 * c, 512 * c + 512)
+            src = mb[j][:, t, cols].bitcast(FP8)
+            if engine == "v":
+                nc.vector.tensor_copy(out=wide[j][:, t, cols], in_=src)
+            else:
+                nc.scalar.copy(out=wide[j][:, t, cols], in_=src)
+
+        wide[0] = work.tile([NP, 2, P], BF16, name="wide0", tag="wide", bufs=3, align_bytes=64)
+        widen_part(0, 0, 0, "v")
+        widen_part(0, 1, 0, "s")
+        widen_part(0, 0, 1, "v")
+        widen_part(0, 1, 1, "v")
+        widen_pair(1)
+        for c in range(NC):
+            turn_mask(0, c)
+        sbank = {}
+        for h in range(2):
+            for c in range(NC):
+                sbank[h, c] = turn(
+                    [scn[2 * h][:].bitcast(F32), scn[2 * h + 1][:].bitcast(F32)], c, f"m{2 * h + c}", f"sb{h}_{c}"
+                )
+        sq = [keep.tile([NP, B, 4], BF16, name=f"sq{c}", align_bytes=64) for c in range(NC)]
+        for h in range(2):
+            for c in range(NC):
+                nc.scalar.copy(
+                    out=sq[c][:, 256 * h : 256 * (h + 1), :].rearrange("p x t -> p (x t)").bitcast(F32).rearrange("p (x u) -> p x u", u=2),
+                    in_=sbank[h, c][:].rearrange("p u x -> p x u"),
+                )
+
+        for j in range(NPAIR):
+            prev = j - 1
+            form = FORM[prev // 2][0] if prev >= 0 else ""
+            if form == "A" and not W_FIRST:
+                subtract_dark(prev, 0)
+                subtract_dark(prev, 1)
+            if j + 2 < NPAIR:
+                widen_pair(j + 2)
+            if form == "A" and W_FIRST:
+                subtract_dark(prev, 0)
+                subtract_dark(prev, 1)
+            for c in range(NC):
+                scale_mask(j, c)
+            if j == 1:
+                for c in range(NC):
+                    nc.vector.quantize_mx(
+                        out=scodes[:, c, :].bitcast(E4M3X4),
+                        scales=sscales[:, c, :],
+                        in_=sq[c][:].rearrange("p x t -> p (x t)"),
+                    )
+            if j == 0:
+                quant_mask(0)
+            if j == 1:
+                quant_mask(1)
+                project(0, 0)
+                project(0, 1)
+            if form == "B":
+                whiten(prev, 0)
+            for g in range(LAST):
+                if j == QZ_STEP[g] and QZ_FIRST[g]:
+                    quant_z(g, 0, B)
+            if j > 1:
+                quant_mask(j)
+            if form == "B":
+                whiten(prev, 1)
+            for g in range(LAST):
+                if j == QZ_STEP[g] and not QZ_FIRST[g]:
+                    quant_z(g, 0, B)
+            if j + 1 < NPAIR:
+                for c in range(NC):
+                    turn_mask(j + 1, c)
+            if j > 0:
+                project(j, 0)
+                project(j, 1)
+            if prev >= 0 and prev % 2 == 1:
+                finish_z(prev // 2)
+            if j == QZ_STEP[0]:
+                early(0)
+            if j == QZ_STEP[1]:
+                early(1)
+                park()
+            if j == max(QZ_STEP[1] + 1, MID_STEP):
+                for m in range(4):
+                    backproject(m, 0)
+                    backproject(m, 1)
+            if j == QZ_STEP[2]:
+                for m in range(6):
+                    backproject(m, 2)
+
+        whiten(NPAIR - 1, 0)
+        whiten(NPAIR - 1, 1)
+        finish_z(LAST)
+        if QZ_STEP[2] == NPAIR:
+            quant_z(2, 0, B)
+            for m in range(6):
+                backproject(m, 2)
+        for m in range(6, NM):
+            backproject(m, 2)
+        quant_z(LAST, 0, 256)
+        quant_z(LAST, 256, B)
+        out_v = out.rearrange("(m p) b -> m p b", p=NP)
+        for m in (0, 4, 1, 5, 2, 6, 3, 7):
+            backproject(m, LAST)
+            res = work.tile([NP, B], F32, name=f"res{m}", tag="res", bufs=8)
+            if m < 4:
+                nc.scalar.copy(out=res[:], in_=img[m][:])
+            else:
+                nc.vector.tensor_tensor(out=res[:], in0=img[m][:], in1=part[m][:], op=ALU.add)
+            nc.sync.dma_start(out=out_v[m], in_=res[:])

@@ -13,8 +13,8 @@ E2M1X4 = mybir.dt.float4_e2m1fn_x4
 ALU = mybir.AluOpType
 
 D, P, B = 2048, 1024, 512
-QZ_STEP = [3, 6, 8]
-QZ_FIRST = [0, 1, 1]
+QZ_STEP = [3, 5, 7]
+QZ_FIRST = [0, 0, 0]
 FLOPS = 2 * 2 * D * P * B
 
 NP = 128
@@ -22,7 +22,7 @@ NG = D // 512
 NPAIR = 2 * NG
 NC = P // 512
 NM = P // 128
-FORM = [("B", 512, 0), ("A", 512), ("A", 512), ("B", 0, 192)]
+FORM = [("B", 0, 512), ("B", 0, 512), ("B", 0, 512), ("B", 0, 192)]
 W_FIRST = True
 G_PIECE = 128
 MID_STEP = 0
@@ -313,12 +313,12 @@ def tile_coded_aperture_backprojection_s13_kernel(
         for j in range(NPAIR):
             prev = j - 1
             form = FORM[prev // 2][0] if prev >= 0 else ""
-            if form == "A" and not W_FIRST:
+            if form == "A" and not W_FIRST and j > 1:
                 subtract_dark(prev, 0)
                 subtract_dark(prev, 1)
             if j + 2 < NPAIR:
                 widen_pair(j + 2)
-            if form == "A" and W_FIRST:
+            if form == "A" and W_FIRST and j > 1:
                 subtract_dark(prev, 0)
                 subtract_dark(prev, 1)
             for c in range(NC):
@@ -334,8 +334,13 @@ def tile_coded_aperture_backprojection_s13_kernel(
                 quant_mask(0)
             if j == 1:
                 quant_mask(1)
+                for c in range(NC):
+                    turn_mask(2, c)
                 project(0, 0)
                 project(0, 1)
+                if FORM[0][0] == "A":
+                    subtract_dark(0, 0)
+                    subtract_dark(0, 1)
             if form == "B":
                 whiten(prev, 0)
             for g in range(LAST):
@@ -348,7 +353,7 @@ def tile_coded_aperture_backprojection_s13_kernel(
             for g in range(LAST):
                 if j == QZ_STEP[g] and not QZ_FIRST[g]:
                     quant_z(g, 0, B)
-            if j + 1 < NPAIR:
+            if j + 1 < NPAIR and j != 1:
                 for c in range(NC):
                     turn_mask(j + 1, c)
             if j > 0:

@@ -22,6 +22,16 @@ NG = D // 512
 NPAIR = 2 * NG
 NC = P // 512
 NM = P // 128
+V_W1 = True
+W2_FIRST = True
+V_SCENES = []
+POOL_PAIRS = (2, 4)
+PIECE = 256
+SEQ = [0, 1, 3, 2, 5, 4, 6, 7]
+WS = [[2], [3], [4], [5], [6], [7], [], [], []]
+FIN = {2: 0, 4: 1, 6: 2}
+ZMID = False
+Q_LATE = False
 FORM = [("B", 0, 512), ("B", 0, 512), ("B", 0, 512), ("B", 0, 192)]
 W_FIRST = True
 G_PIECE = 128
@@ -61,6 +71,7 @@ def tile_coded_aperture_backprojection_s13_kernel(
         scn_v = scenes.rearrange("(r p) k -> r p k", p=NP)
 
         mb = [keep.tile([NP, 2, P], U8, name=f"mb{j}", align_bytes=64) for j in range(NPAIR)]
+        srow = keep.tile([NP, P], F32, name="srow")
         sig = [keep.tile([NP, 4, B], BF16, name=f"sig{g}", align_bytes=64) for g in range(NG)]
         scn = [keep.tile([NP, P], BF16, name=f"scn{r}", align_bytes=64) for r in range(4)]
         gw = [keep.tile([NP, 2 * P], U8, name=f"gw{g}", align_bytes=64) for g in range(NG)]
@@ -72,9 +83,13 @@ def tile_coded_aperture_backprojection_s13_kernel(
         for j in range(2):
             for t in range(2):
                 nc.sync.dma_start(out=mb[j][:, t, :], in_=mask_v[0][:, 2 * j + t, :])
+        if W2_FIRST:
+            load_mask(2)
         for r in range(4):
             nc.sync.dma_start(out=scn[r][:], in_=scn_v[r])
-        load_mask(2)
+        if not W2_FIRST:
+            load_mask(2)
+        nc.sync.dma_start(out=srow[:], in_=mask_scale.rearrange("o k -> (o k)").partition_broadcast(NP))
         nc.sync.dma_start(out=sig[0][:], in_=sig_v[0])
         for j in range(3, 8):
             load_mask(j)
@@ -112,7 +127,7 @@ def tile_coded_aperture_backprojection_s13_kernel(
 
         def widen(j, t, engine):
             if t == 0:
-                wide[j] = work.tile([NP, 2, P], BF16, name=f"wide{j}", tag="wide", bufs=3, align_bytes=64)
+                wide[j] = work.tile([NP, 2, P], BF16, name=f"wide{j}", tag="wide", bufs=5, align_bytes=64)
             src = mb[j][:, t, :].bitcast(FP8)
             if engine == "v":
                 nc.vector.tensor_copy(out=wide[j][:, t, :], in_=src)
@@ -120,7 +135,7 @@ def tile_coded_aperture_backprojection_s13_kernel(
                 nc.scalar.copy(out=wide[j][:, t, :], in_=src)
 
         def widen_pair(j):
-            wide[j] = work.tile([NP, 2, P], BF16, name=f"wide{j}", tag="wide", bufs=3, align_bytes=64)
+            wide[j] = work.tile([NP, 2, P], BF16, name=f"wide{j}", tag="wide", bufs=5, align_bytes=64)
             nc.scalar.copy(
                 out=wide[j][:].rearrange("p t k -> p (t k)"), in_=mb[j][:].rearrange("p t k -> p (t k)").bitcast(FP8)
             )
@@ -140,7 +155,7 @@ def tile_coded_aperture_backprojection_s13_kernel(
 
         def scale_mask(j, c):
             if c == 0:
-                qin[j] = work.tile([NP, NC, 256, 4], BF16, name=f"qin{j}", tag="qin", bufs=2, align_bytes=64)
+                qin[j] = work.tile([NP, NC, 256, 4], BF16, name=f"qin{j}", tag="qin", bufs=3, align_bytes=64)
             nc.vector.tensor_tensor(
                 out=qin[j][:, c].rearrange("p x (u e) -> p x u e", u=2),
                 in0=tbank[j, c][:].bitcast(BF16).rearrange("p u (x e) -> p x u e", e=2),
@@ -148,9 +163,29 @@ def tile_coded_aperture_backprojection_s13_kernel(
                 op=ALU.mult,
             )
 
+        def pool_product(j):
+            if j not in POOL_PAIRS:
+                return
+            prod = work.tile([NP, 2, P], BF16, name=f"prod{j}", tag="prod", bufs=2, align_bytes=64)
+            for t in range(2):
+                for k0 in range(0, P, PIECE):
+                    cols = slice(k0, k0 + PIECE)
+                    nc.gpsimd.tensor_tensor(
+                        out=prod[:, t, cols], in0=wide[j][:, t, cols], in1=srow[:, cols], op=ALU.mult
+                    )
+            wide[j] = prod
+
+        def copy_words(j, c):
+            if c == 0:
+                qin[j] = work.tile([NP, NC, 256, 4], BF16, name=f"qin{j}", tag="qin", bufs=3, align_bytes=64)
+            nc.scalar.copy(
+                out=qin[j][:, c].rearrange("p x t -> p (x t)").bitcast(F32).rearrange("p (x u) -> p x u", u=2),
+                in_=tbank[j, c][:].rearrange("p u x -> p x u"),
+            )
+
         def quant_mask(j):
-            codes[j] = work.tile([NP, NC, 256], U32, name=f"codes{j}", tag="codes", bufs=3, align_bytes=64)
-            scales[j] = work.tile([NP, NC, 256], U8, name=f"scales{j}", tag="scales", bufs=3, align_bytes=64)
+            codes[j] = work.tile([NP, NC, 256], U32, name=f"codes{j}", tag="codes", bufs=4, align_bytes=64)
+            scales[j] = work.tile([NP, NC, 256], U8, name=f"scales{j}", tag="scales", bufs=4, align_bytes=64)
             nc.vector.quantize_mx(
                 out=codes[j][:].rearrange("p c x -> p (c x)").bitcast(E4M3X4),
                 scales=scales[j][:].rearrange("p c x -> p (c x)"),
@@ -174,7 +209,7 @@ def tile_coded_aperture_backprojection_s13_kernel(
         def whiten(j, t):
             g, h = divmod(j, 2)
             s = 2 * h + t
-            if s == 0:
+            if g not in zt:
                 zt[g] = work.tile([NP, 4, B], BF16, name=f"zt{g}", tag="zt", bufs=2, align_bytes=64)
             nc.vector.scalar_tensor_tensor(
                 out=zt[g][:, s, :],
@@ -288,99 +323,148 @@ def tile_coded_aperture_backprojection_s13_kernel(
             else:
                 nc.scalar.copy(out=wide[j][:, t, cols], in_=src)
 
-        wide[0] = work.tile([NP, 2, P], BF16, name="wide0", tag="wide", bufs=3, align_bytes=64)
+        wide[0] = work.tile([NP, 2, P], BF16, name="wide0", tag="wide", bufs=5, align_bytes=64)
         widen_part(0, 0, 0, "v")
         widen_part(0, 1, 0, "s")
         widen_part(0, 0, 1, "v")
         widen_part(0, 1, 1, "v")
-        widen_pair(1)
+        if V_W1:
+            wide[1] = work.tile([NP, 2, P], BF16, name="wide1", tag="wide", bufs=5, align_bytes=64)
+            widen_part(1, 0, 0, "v")
+            widen_part(1, 0, 1, "s")
+            widen(1, 1, "s")
+        else:
+            widen_pair(1)
         for c in range(NC):
             turn_mask(0, c)
         sbank = {}
-        for h in range(2):
+        sq = [keep.tile([NP, B, 4], BF16, name=f"sq{c}", align_bytes=64) for c in range(NC)]
+
+        def turn_scenes(h):
             for c in range(NC):
                 sbank[h, c] = turn(
                     [scn[2 * h][:].bitcast(F32), scn[2 * h + 1][:].bitcast(F32)], c, f"m{2 * h + c}", f"sb{h}_{c}"
                 )
-        sq = [keep.tile([NP, B, 4], BF16, name=f"sq{c}", align_bytes=64) for c in range(NC)]
+
+        def empty_scenes(h, c):
+            dst = sq[c][:, 256 * h : 256 * (h + 1), :].rearrange("p x t -> p (x t)").bitcast(F32).rearrange("p (x u) -> p x u", u=2)
+            src = sbank[h, c][:].rearrange("p u x -> p x u")
+            if (h, c) in V_SCENES:
+                nc.vector.tensor_copy(out=dst, in_=src)
+            else:
+                nc.scalar.copy(out=dst, in_=src)
+
+        def quant_scenes(c):
+            nc.vector.quantize_mx(
+                out=scodes[:, c, :].bitcast(E4M3X4),
+                scales=sscales[:, c, :],
+                in_=sq[c][:].rearrange("p x t -> p (x t)"),
+            )
+
+        def product(j, c):
+            if j in POOL_PAIRS:
+                copy_words(j, c)
+            else:
+                scale_mask(j, c)
+
+        def turn_pair(j):
+            turn_mask(j, 0)
+            turn_mask(j, 1)
+
+        def project_pair(j):
+            project(j, 0)
+            project(j, 1)
+
+        turn_scenes(0)
+        scale_mask(0, 0)
+        turn_mask(1, 0)
+        scale_mask(0, 1)
+        turn_mask(1, 1)
+        turn_scenes(1)
+        widen_pair(2)
+        pool_product(2)
         for h in range(2):
             for c in range(NC):
-                nc.scalar.copy(
-                    out=sq[c][:, 256 * h : 256 * (h + 1), :].rearrange("p x t -> p (x t)").bitcast(F32).rearrange("p (x u) -> p x u", u=2),
-                    in_=sbank[h, c][:].rearrange("p u x -> p x u"),
-                )
-
-        for j in range(NPAIR):
-            prev = j - 1
-            form = FORM[prev // 2][0] if prev >= 0 else ""
-            if form == "A" and not W_FIRST and j > 1:
-                subtract_dark(prev, 0)
-                subtract_dark(prev, 1)
-            if j + 2 < NPAIR:
-                widen_pair(j + 2)
-            if form == "A" and W_FIRST and j > 1:
-                subtract_dark(prev, 0)
-                subtract_dark(prev, 1)
-            for c in range(NC):
-                scale_mask(j, c)
-            if j == 1:
-                for c in range(NC):
-                    nc.vector.quantize_mx(
-                        out=scodes[:, c, :].bitcast(E4M3X4),
-                        scales=sscales[:, c, :],
-                        in_=sq[c][:].rearrange("p x t -> p (x t)"),
-                    )
-            if j == 0:
-                quant_mask(0)
-            if j == 1:
-                quant_mask(1)
-                for c in range(NC):
-                    turn_mask(2, c)
-                project(0, 0)
-                project(0, 1)
-                if FORM[0][0] == "A":
-                    subtract_dark(0, 0)
-                    subtract_dark(0, 1)
-            if form == "B":
-                whiten(prev, 0)
-            for g in range(LAST):
-                if j == QZ_STEP[g] and QZ_FIRST[g]:
-                    quant_z(g, 0, B)
-            if j > 1:
-                quant_mask(j)
-            if form == "B":
-                whiten(prev, 1)
-            for g in range(LAST):
-                if j == QZ_STEP[g] and not QZ_FIRST[g]:
-                    quant_z(g, 0, B)
-            if j + 1 < NPAIR and j != 1:
-                for c in range(NC):
-                    turn_mask(j + 1, c)
-            if j > 0:
-                project(j, 0)
-                project(j, 1)
-            if prev >= 0 and prev % 2 == 1:
-                finish_z(prev // 2)
-            if j == QZ_STEP[0]:
-                early(0)
-            if j == QZ_STEP[1]:
-                early(1)
-                park()
-            if j == max(QZ_STEP[1] + 1, MID_STEP):
-                for m in range(4):
-                    backproject(m, 0)
-                    backproject(m, 1)
-            if j == QZ_STEP[2]:
-                for m in range(6):
-                    backproject(m, 2)
+                empty_scenes(h, c)
+        scale_mask(1, 0)
+        quant_mask(0)
+        scale_mask(1, 1)
+        quant_scenes(0)
+        quant_scenes(1)
+        quant_mask(1)
+        widen_pair(3)
+        project_pair(0)
+        whiten(0, 0)
+        whiten(0, 1)
+        turn_pair(3)
+        project_pair(1)
+        widen_pair(5)
+        widen_pair(4)
+        pool_product(4)
+        scale_mask(3, 0)
+        scale_mask(3, 1)
+        whiten(1, 0)
+        quant_mask(3)
+        whiten(1, 1)
+        turn_pair(2)
+        project_pair(3)
+        copy_words(2, 0)
+        copy_words(2, 1)
+        widen_pair(6)
+        whiten(3, 0)
+        quant_mask(2)
+        whiten(3, 1)
+        turn_pair(5)
+        project_pair(2)
+        interleave(0, 0, 256, "s")
+        scale_mask(5, 0)
+        whiten(2, 0)
+        scale_mask(5, 1)
+        whiten(2, 1)
+        quant_mask(5)
+        turn_pair(4)
+        copy_words(4, 0)
+        interleave(0, 256, B, "s")
+        copy_words(4, 1)
+        quant_z(0, 0, B)
+        quant_mask(4)
+        turn_pair(6)
+        project_pair(5)
+        early(0)
+        interleave(1, 0, 256, "s")
+        interleave(1, 256, B, "s")
+        scale_mask(6, 0)
+        whiten(5, 0)
+        scale_mask(6, 1)
+        whiten(5, 1)
+        project_pair(4)
+        quant_z(1, 0, B)
+        early(1)
+        widen_pair(7)
+        park()
+        whiten(4, 0)
+        quant_mask(6)
+        whiten(4, 1)
+        turn_pair(7)
+        project_pair(6)
+        for g in range(2):
+            for m in range(4):
+                backproject(m, g)
+        interleave(2, 0, 256, "s")
+        interleave(2, 256, B, "s")
+        scale_mask(7, 0)
+        whiten(6, 0)
+        scale_mask(7, 1)
+        quant_z(2, 0, B)
+        quant_mask(7)
+        whiten(6, 1)
+        project_pair(7)
+        for m in range(6):
+            backproject(m, 2)
 
         whiten(NPAIR - 1, 0)
         whiten(NPAIR - 1, 1)
         finish_z(LAST)
-        if QZ_STEP[2] == NPAIR:
-            quant_z(2, 0, B)
-            for m in range(6):
-                backproject(m, 2)
         for m in range(6, NM):
             backproject(m, 2)
         quant_z(LAST, 0, 256)

@@ -11,10 +11,9 @@ FP8 = mybir.dt.float8_e4m3fn
 E4M3X4 = mybir.dt.float8_e4m3fn_x4
 E2M1X4 = mybir.dt.float4_e2m1fn_x4
 ALU = mybir.AluOpType
+COPY = mybir.ActivationFunctionType.Copy
 
 D, P, B = 2048, 1024, 512
-QZ_STEP = [3, 5, 7]
-QZ_FIRST = [0, 0, 0]
 FLOPS = 2 * 2 * D * P * B
 
 NP = 128
@@ -22,56 +21,43 @@ NG = D // 512
 NPAIR = 2 * NG
 NC = P // 512
 NM = P // 128
-V_W1 = True
-W2_FIRST = True
-V_SCENES = []
-POOL_PAIRS = (2, 4)
-PIECE = 256
-SEQ = [0, 1, 3, 2, 5, 4, 6, 7]
-WS = [[2], [3], [4], [5], [6], [7], [], [], []]
-FIN = {2: 0, 4: 1, 6: 2}
-ZMID = False
-Q_LATE = False
-FORM = [("B", 0, 512), ("B", 0, 512), ("B", 0, 512), ("B", 0, 192)]
-W_FIRST = True
-G_PIECE = 128
-MID_STEP = 0
+S_UNITS = []
+WARM0 = 6
+WARM1 = 1
+WC0 = 0
+WC1 = 1
+SPLIT = 1
 
 
 def tile_coded_aperture_backprojection_s13_kernel(
     tc, mask_bytes, mask_scale, scenes, dark, inv_sigma, dec_words, dec_scales, out
 ):
     nc = tc.nc
-    with ExitStack() as ctx:
+    with ExitStack() as ctx, tc.manual_schedule():
         keep = ctx.enter_context(tc.tile_pool(name="keep", bufs=1))
         work = ctx.enter_context(tc.tile_pool(name="work", bufs=2))
         psum = ctx.enter_context(tc.psum_pool(name="psum", bufs=1))
-        ctx.enter_context(tc.manual_schedule())
 
-        dummy = keep.tile([NP, 2], F32, name="dummy")
-        nc.vector.memset(dummy[:], 0.0)
-        nc.scalar.copy(out=dummy[:, 1:2], in_=dummy[:, 0:1])
-
+        zeros = keep.tile([NP, 512], BF16, name="zeros")
+        nc.vector.memset(zeros[:], 0.0)
         mscale = keep.tile([NP, NC, 2, 2], F32, name="mscale")
         nc.scalar.dma_start(
             out=mscale[:], in_=mask_scale.rearrange("o (c p u e) -> p (o c) u e", c=NC, p=NP, u=2, e=2)
         )
+        first = keep.tile([NP, 2], BF16, name="first")
+        nc.scalar.copy(out=first[:], in_=zeros[:, 0:2])
+        darks = keep.tile([NP, NG, 4], BF16, name="darks")
+        nc.scalar.dma_start(out=darks[:], in_=dark.rearrange("(g p t) -> p g t", g=NG, p=NP, t=4))
         ident = keep.tile([NP, NP], F32, name="ident")
         make_identity(nc, ident[:])
         gsc = keep.tile([NP, NG, P], U8, name="gsc", align_bytes=64)
         nc.gpsimd.memset(gsc[:].bitcast(I32), 0)
-        darks = keep.tile([NP, NG, 4], BF16, name="darks")
-        nc.gpsimd.dma_start(out=darks[:], in_=dark.rearrange("(g p t) -> p g t", g=NG, p=NP, t=4))
-
-        negd = keep.tile([NP, NG, 4], F32, name="negd")
-        nc.gpsimd.tensor_scalar(out=negd[:], in0=darks[:], scalar1=-1.0, scalar2=None, op0=ALU.mult)
 
         mask_v = mask_bytes.rearrange("(g p t) k -> g p t k", g=NG, p=NP, t=4)
         sig_v = inv_sigma.rearrange("(g p t) b -> g p t b", g=NG, p=NP, t=4)
         scn_v = scenes.rearrange("(r p) k -> r p k", p=NP)
 
         mb = [keep.tile([NP, 2, P], U8, name=f"mb{j}", align_bytes=64) for j in range(NPAIR)]
-        srow = keep.tile([NP, P], F32, name="srow")
         sig = [keep.tile([NP, 4, B], BF16, name=f"sig{g}", align_bytes=64) for g in range(NG)]
         scn = [keep.tile([NP, P], BF16, name=f"scn{r}", align_bytes=64) for r in range(4)]
         gw = [keep.tile([NP, 2 * P], U8, name=f"gw{g}", align_bytes=64) for g in range(NG)]
@@ -83,17 +69,16 @@ def tile_coded_aperture_backprojection_s13_kernel(
         for j in range(2):
             for t in range(2):
                 nc.sync.dma_start(out=mb[j][:, t, :], in_=mask_v[0][:, 2 * j + t, :])
-        if W2_FIRST:
-            load_mask(2)
-        for r in range(4):
+        for r in range(2):
             nc.sync.dma_start(out=scn[r][:], in_=scn_v[r])
-        if not W2_FIRST:
-            load_mask(2)
-        nc.sync.dma_start(out=srow[:], in_=mask_scale.rearrange("o k -> (o k)").partition_broadcast(NP))
+        load_mask(2)
+        for r in range(2, 4):
+            nc.sync.dma_start(out=scn[r][:], in_=scn_v[r])
+        load_mask(3)
         nc.sync.dma_start(out=sig[0][:], in_=sig_v[0])
-        for j in range(3, 8):
+        for j in range(4, 8):
             load_mask(j)
-            if j % 2 == 0:
+            if j % 2 == 1:
                 nc.sync.dma_start(out=sig[j // 2 - 1][:], in_=sig_v[j // 2 - 1])
         nc.sync.dma_start(out=sig[3][:], in_=sig_v[3])
         for q in range(4):
@@ -108,6 +93,7 @@ def tile_coded_aperture_backprojection_s13_kernel(
         sscales = keep.tile([NP, NC, B], U8, name="sscales", align_bytes=64)
         zcodes = [keep.tile([NP, B], U32, name=f"zcodes{g}", align_bytes=64) for g in range(NG)]
         zscales = [keep.tile([NP, B], U8, name=f"zscales{g}", align_bytes=64) for g in range(NG)]
+        sq = [keep.tile([NP, B, 4], BF16, name=f"sq{c}", align_bytes=64) for c in range(NC)]
 
         wide = {}
         tbank = {}
@@ -116,72 +102,91 @@ def tile_coded_aperture_backprojection_s13_kernel(
         scales = {}
         ybank = {}
         zt = {}
-        ysb = {}
         zq = {}
         img = {}
         part = {}
+        pbank = {}
+        sbank = {}
 
         def bank(tag, shape, name):
             t = psum.tile(shape, F32, name=name, tag=tag)
             return t
 
-        def widen(j, t, engine):
-            if t == 0:
-                wide[j] = work.tile([NP, 2, P], BF16, name=f"wide{j}", tag="wide", bufs=5, align_bytes=64)
-            src = mb[j][:, t, :].bitcast(FP8)
+        def warm(bk, n):
+            for i in range(n):
+                nc.tensor.matmul(out=bk, lhsT=zeros[:, 0:128], rhs=zeros[:], start=True, stop=True)
+
+        def widen(j, t, c0, c1, engine):
+            if j not in wide:
+                wide[j] = work.tile([NP, 2, P], BF16, name=f"wide{j}", tag="wide", bufs=4, align_bytes=64)
+            src = mb[j][:, t, c0:c1].bitcast(FP8)
             if engine == "v":
-                nc.vector.tensor_copy(out=wide[j][:, t, :], in_=src)
+                nc.vector.tensor_copy(out=wide[j][:, t, c0:c1], in_=src)
             else:
-                nc.scalar.copy(out=wide[j][:, t, :], in_=src)
+                nc.scalar.copy(out=wide[j][:, t, c0:c1], in_=src)
 
         def widen_pair(j):
-            wide[j] = work.tile([NP, 2, P], BF16, name=f"wide{j}", tag="wide", bufs=5, align_bytes=64)
+            wide[j] = work.tile([NP, 2, P], BF16, name=f"wide{j}", tag="wide", bufs=4, align_bytes=64)
             nc.scalar.copy(
                 out=wide[j][:].rearrange("p t k -> p (t k)"), in_=mb[j][:].rearrange("p t k -> p (t k)").bitcast(FP8)
             )
 
-        def turn(tiles, c, tag, name):
-            bk = bank(tag, [NP, 2, 256], name)
+        def turn(bk, tiles, c):
             for t in range(2):
                 for u in range(2):
                     nc.tensor.transpose(
                         bk[:, u, 128 * t : 128 * t + 128], tiles[t][:, 256 * c + u : 256 * (c + 1) : 2], ident[:]
                     )
-            return bk
 
-        def turn_mask(j, c):
+        def turn_mask(j, c, n=0):
             w = wide[j][:].bitcast(F32)
-            tbank[j, c] = turn([w[:, 0, :], w[:, 1, :]], c, f"t{c}", f"tb{j}_{c}")
+            bk = bank(f"t{c}", [NP, 2, 256], f"tb{j}_{c}")
+            tbank[j, c] = bk
+            warm(bk[:].rearrange("p u x -> p (u x)"), n)
+            turn(bk, [w[:, 0, :], w[:, 1, :]], c)
 
-        def scale_mask(j, c):
-            if c == 0:
+        def turn_scenes(h, c, n=0):
+            bk = bank(f"m{2 * h + c}", [NP, 2, 256], f"sb{h}_{c}")
+            sbank[h, c] = bk
+            warm(bk[:].rearrange("p u x -> p (u x)"), n)
+            turn(bk, [scn[2 * h][:].bitcast(F32), scn[2 * h + 1][:].bitcast(F32)], c)
+
+        def empty_scenes(h, c):
+            dst = sq[c][:, 256 * h : 256 * (h + 1), :].rearrange("p x t -> p (x t)").bitcast(F32)
+            nc.scalar.copy(
+                out=dst.rearrange("p (x u) -> p x u", u=2), in_=sbank[h, c][:].rearrange("p u x -> p x u")
+            )
+
+        def quant_scenes(c):
+            nc.vector.quantize_mx(
+                out=scodes[:, c, :].bitcast(E4M3X4),
+                scales=sscales[:, c, :],
+                in_=sq[c][:].rearrange("p x t -> p (x t)"),
+            )
+
+        def product(j, c):
+            if j not in qin:
                 qin[j] = work.tile([NP, NC, 256, 4], BF16, name=f"qin{j}", tag="qin", bufs=3, align_bytes=64)
+            src = tbank[j, c][:].bitcast(BF16).rearrange("p u (x e) -> p x u e", e=2)
+            if (j, c) in S_UNITS:
+                scale_mask_scalar(src, j, c)
+                return
             nc.vector.tensor_tensor(
                 out=qin[j][:, c].rearrange("p x (u e) -> p x u e", u=2),
-                in0=tbank[j, c][:].bitcast(BF16).rearrange("p u (x e) -> p x u e", e=2),
+                in0=src,
                 in1=mscale[:, c : c + 1].to_broadcast([NP, 256, 2, 2]),
                 op=ALU.mult,
             )
 
-        def pool_product(j):
-            if j not in POOL_PAIRS:
-                return
-            prod = work.tile([NP, 2, P], BF16, name=f"prod{j}", tag="prod", bufs=2, align_bytes=64)
-            for t in range(2):
-                for k0 in range(0, P, PIECE):
-                    cols = slice(k0, k0 + PIECE)
-                    nc.gpsimd.tensor_tensor(
-                        out=prod[:, t, cols], in0=wide[j][:, t, cols], in1=srow[:, cols], op=ALU.mult
+        def scale_mask_scalar(src, j, c):
+            for u in range(2):
+                for e in range(2):
+                    nc.scalar.activation(
+                        out=qin[j][:, c, :, 2 * u + e],
+                        in_=src[:, :, u, e],
+                        func=COPY,
+                        scale=mscale[:, c, u, e : e + 1],
                     )
-            wide[j] = prod
-
-        def copy_words(j, c):
-            if c == 0:
-                qin[j] = work.tile([NP, NC, 256, 4], BF16, name=f"qin{j}", tag="qin", bufs=3, align_bytes=64)
-            nc.scalar.copy(
-                out=qin[j][:, c].rearrange("p x t -> p (x t)").bitcast(F32).rearrange("p (x u) -> p x u", u=2),
-                in_=tbank[j, c][:].rearrange("p u x -> p x u"),
-            )
 
         def quant_mask(j):
             codes[j] = work.tile([NP, NC, 256], U32, name=f"codes{j}", tag="codes", bufs=4, align_bytes=64)
@@ -220,62 +225,17 @@ def tile_coded_aperture_backprojection_s13_kernel(
                 op1=ALU.mult,
             )
 
-        def subtract_dark(j, t):
-            g, h = divmod(j, 2)
-            s = 2 * h + t
-            if s == 0:
-                ysb[g] = work.tile([NP, 4, B], F32, name=f"ysb{g}", tag="ysb", bufs=2, align_bytes=64)
-            nc.scalar.activation(
-                out=ysb[g][:, s, :],
-                in_=ybank[j, t][:],
-                func=mybir.ActivationFunctionType.Identity,
-                bias=negd[:, g, s : s + 1],
-                scale=1.0,
-            )
-
-        def weigh(g, b0, b1, engine):
-            if b0 == 0:
-                zq[g] = work.tile([NP, B, 4], BF16, name=f"zq{g}", tag="zq", bufs=2, align_bytes=64)
-            engine.tensor_tensor(
-                out=zq[g][:, b0:b1, :],
-                in0=ysb[g][:, :, b0:b1].rearrange("p t b -> p b t"),
-                in1=sig[g][:, :, b0:b1].rearrange("p t b -> p b t"),
-                op=ALU.mult,
-            )
-
         def interleave(g, b0, b1, engine):
-            if b0 == 0:
+            if g not in zq:
                 zq[g] = work.tile([NP, B, 4], BF16, name=f"zq{g}", tag="zq", bufs=2, align_bytes=64)
-            dst = zq[g][:, b0:b1, :]
-            src = zt[g][:, :, b0:b1].rearrange("p t b -> p b t")
+            dst = zq[g][:, b0:b1, :].rearrange("p (c i) t -> p c t i", i=4)
+            src = zt[g][:, :, b0:b1].rearrange("p t (c i) -> p c t i", i=4)
             if engine == "v":
                 nc.vector.tensor_copy(out=dst, in_=src)
-            elif engine == "g":
-                nc.gpsimd.tensor_scalar(out=dst, in0=src, scalar1=1.0, scalar2=0.0, op0=ALU.mult, op1=ALU.add)
             else:
                 nc.scalar.copy(out=dst, in_=src)
 
-        def finish_z(g):
-            form = FORM[g]
-            if form[0] == "A":
-                for b0 in range(0, form[1], G_PIECE):
-                    weigh(g, b0, b0 + G_PIECE, nc.gpsimd)
-                if form[1] < B:
-                    weigh(g, form[1], B, nc.vector)
-            else:
-                b0 = 0
-                while b0 < form[1]:
-                    interleave(g, b0, b0 + 128, "g")
-                    b0 += 128
-                if form[2]:
-                    n = 1 if form[2] <= 256 else 2
-                    for i in range(n):
-                        interleave(g, b0, b0 + form[2] // n, "s")
-                        b0 += form[2] // n
-                if b0 < B:
-                    interleave(g, b0, B, "v")
-
-        def quant_z(g, b0, b1):
+        def quant_z(g, b0=0, b1=B):
             nc.vector.quantize_mx(
                 out=zcodes[g][:, b0:b1].bitcast(E4M3X4),
                 scales=zscales[g][:, b0:b1],
@@ -296,176 +256,111 @@ def tile_coded_aperture_backprojection_s13_kernel(
                 stop=stop,
             )
 
-        pbank = {}
+        def early(m, g):
+            if g == 0:
+                pbank[m] = bank(f"m{m - 4}", [NP, B], f"early{m}")
+            image_pass(pbank[m], m, g, g == 0, g == 1)
 
-        def early(g):
-            for m in range(4, NM):
-                if g == 0:
-                    pbank[m] = bank(f"m{m - 4}", [NP, B], f"early{m}")
-                image_pass(pbank[m], m, g, g == 0, g == 1)
-
-        def park():
-            for m in range(4, NM):
-                part[m] = keep.tile([NP, B], F32, name=f"part{m}")
-                nc.scalar.copy(out=part[m][:], in_=pbank[m][:])
+        def park(m):
+            part[m] = keep.tile([NP, B], F32, name=f"part{m}")
+            nc.scalar.copy(out=part[m][:], in_=pbank[m][:])
 
         def backproject(m, g):
-            first = 0 if m < 4 else 2
-            if g == first:
+            g0 = 0 if m < 4 else 2
+            if g == g0:
                 img[m] = bank(IMG_TAG[m], [NP, B], f"img{m}")
-            image_pass(img[m], m, g, g == first, g == LAST)
+            image_pass(img[m], m, g, g == g0, g == LAST)
 
-        def widen_part(j, t, c, engine):
-            cols = slice(512 * c, 512 * c + 512)
-            src = mb[j][:, t, cols].bitcast(FP8)
-            if engine == "v":
-                nc.vector.tensor_copy(out=wide[j][:, t, cols], in_=src)
-            else:
-                nc.scalar.copy(out=wide[j][:, t, cols], in_=src)
-
-        wide[0] = work.tile([NP, 2, P], BF16, name="wide0", tag="wide", bufs=5, align_bytes=64)
-        widen_part(0, 0, 0, "v")
-        widen_part(0, 1, 0, "s")
-        widen_part(0, 0, 1, "v")
-        widen_part(0, 1, 1, "v")
-        if V_W1:
-            wide[1] = work.tile([NP, 2, P], BF16, name="wide1", tag="wide", bufs=5, align_bytes=64)
-            widen_part(1, 0, 0, "v")
-            widen_part(1, 0, 1, "s")
-            widen(1, 1, "s")
-        else:
-            widen_pair(1)
-        for c in range(NC):
-            turn_mask(0, c)
-        sbank = {}
-        sq = [keep.tile([NP, B, 4], BF16, name=f"sq{c}", align_bytes=64) for c in range(NC)]
-
-        def turn_scenes(h):
-            for c in range(NC):
-                sbank[h, c] = turn(
-                    [scn[2 * h][:].bitcast(F32), scn[2 * h + 1][:].bitcast(F32)], c, f"m{2 * h + c}", f"sb{h}_{c}"
-                )
-
-        def empty_scenes(h, c):
-            dst = sq[c][:, 256 * h : 256 * (h + 1), :].rearrange("p x t -> p (x t)").bitcast(F32).rearrange("p (x u) -> p x u", u=2)
-            src = sbank[h, c][:].rearrange("p u x -> p x u")
-            if (h, c) in V_SCENES:
-                nc.vector.tensor_copy(out=dst, in_=src)
-            else:
-                nc.scalar.copy(out=dst, in_=src)
-
-        def quant_scenes(c):
-            nc.vector.quantize_mx(
-                out=scodes[:, c, :].bitcast(E4M3X4),
-                scales=sscales[:, c, :],
-                in_=sq[c][:].rearrange("p x t -> p (x t)"),
-            )
-
-        def product(j, c):
-            if j in POOL_PAIRS:
-                copy_words(j, c)
-            else:
-                scale_mask(j, c)
-
-        def turn_pair(j):
-            turn_mask(j, 0)
-            turn_mask(j, 1)
-
-        def project_pair(j):
-            project(j, 0)
-            project(j, 1)
-
-        turn_scenes(0)
-        scale_mask(0, 0)
-        turn_mask(1, 0)
-        scale_mask(0, 1)
+        wb = bank("y0", [NP, B], "warmbank")
+        warm(wb[:], WARM0)
+        widen(0, 0, 0, 512, "v")
+        widen(0, 1, 0, 512, "s")
+        widen(0, 0, 512, P, "v")
+        widen(0, 1, 512, P, "v")
+        widen(1, 0, 0, 512, "v")
+        widen(1, 0, 512, P, "s")
+        widen(1, 1, 0, P, "s")
+        turn_mask(0, 0)
+        turn_mask(0, 1)
+        product(0, 0)
+        turn_scenes(0, 0, WARM1)
+        turn_scenes(0, 1)
+        turn_mask(1, 0, WARM1)
+        product(0, 1)
         turn_mask(1, 1)
-        turn_scenes(1)
-        widen_pair(2)
-        pool_product(2)
-        for h in range(2):
-            for c in range(NC):
-                empty_scenes(h, c)
-        scale_mask(1, 0)
         quant_mask(0)
-        scale_mask(1, 1)
+        empty_scenes(0, 0)
+        empty_scenes(0, 1)
+        widen_pair(2)
+        turn_scenes(1, 0, WARM1)
+        turn_scenes(1, 1)
+        empty_scenes(1, 0)
+        empty_scenes(1, 1)
+        product(1, 0)
+        turn_mask(2, 0, WARM1)
+        product(1, 1)
+        turn_mask(2, 1)
         quant_scenes(0)
         quant_scenes(1)
-        quant_mask(1)
         widen_pair(3)
-        project_pair(0)
-        whiten(0, 0)
-        whiten(0, 1)
-        turn_pair(3)
-        project_pair(1)
-        widen_pair(5)
-        widen_pair(4)
-        pool_product(4)
-        scale_mask(3, 0)
-        scale_mask(3, 1)
-        whiten(1, 0)
-        quant_mask(3)
-        whiten(1, 1)
-        turn_pair(2)
-        project_pair(3)
-        copy_words(2, 0)
-        copy_words(2, 1)
-        widen_pair(6)
-        whiten(3, 0)
-        quant_mask(2)
-        whiten(3, 1)
-        turn_pair(5)
-        project_pair(2)
-        interleave(0, 0, 256, "s")
-        scale_mask(5, 0)
-        whiten(2, 0)
-        scale_mask(5, 1)
-        whiten(2, 1)
-        quant_mask(5)
-        turn_pair(4)
-        copy_words(4, 0)
-        interleave(0, 256, B, "s")
-        copy_words(4, 1)
-        quant_z(0, 0, B)
-        quant_mask(4)
-        turn_pair(6)
-        project_pair(5)
-        early(0)
-        interleave(1, 0, 256, "s")
-        interleave(1, 256, B, "s")
-        scale_mask(6, 0)
-        whiten(5, 0)
-        scale_mask(6, 1)
-        whiten(5, 1)
-        project_pair(4)
-        quant_z(1, 0, B)
-        early(1)
-        widen_pair(7)
-        park()
-        whiten(4, 0)
-        quant_mask(6)
-        whiten(4, 1)
-        turn_pair(7)
-        project_pair(6)
-        for g in range(2):
-            for m in range(4):
-                backproject(m, g)
-        interleave(2, 0, 256, "s")
-        interleave(2, 256, B, "s")
-        scale_mask(7, 0)
-        whiten(6, 0)
-        scale_mask(7, 1)
-        quant_z(2, 0, B)
-        quant_mask(7)
-        whiten(6, 1)
-        project_pair(7)
-        for m in range(6):
-            backproject(m, 2)
+        quant_mask(1)
+        project(0, 0)
+        project(0, 1)
+
+        for j in range(2, NPAIR):
+            if j == 6:
+                for m in range(4, NM):
+                    early(m, 1)
+            product(j, 0)
+            if j == 2:
+                whiten(0, 0)
+                project(1, 0)
+            if j + 1 < NPAIR:
+                turn_mask(j + 1, 0, WC0)
+            product(j, 1)
+            if j == 2:
+                whiten(0, 1)
+            if j == 2 or SPLIT:
+                project(j - 1, 1)
+            if j == 4:
+                early(4, 0)
+                early(5, 0)
+            if j + 1 < NPAIR:
+                turn_mask(j + 1, 1, WC1)
+            if j + 2 < NPAIR:
+                widen_pair(j + 2)
+            if j == 6:
+                for m in range(4, NM):
+                    park(m)
+            whiten(j - 1, 0)
+            quant_mask(j)
+            whiten(j - 1, 1)
+            if j == 4:
+                early(6, 0)
+                early(7, 0)
+            if j == NPAIR - 1:
+                for m in range(2):
+                    backproject(m, 0)
+                    backproject(m, 1)
+            project(j, 0)
+            if not SPLIT or j == NPAIR - 1:
+                project(j, 1)
+            if j == 6:
+                for m in range(2, 4):
+                    backproject(m, 0)
+                    backproject(m, 1)
+            if j % 2 == 0:
+                g = j // 2 - 1
+                interleave(g, 0, 256, "s")
+                interleave(g, 256, B, "s")
+            else:
+                quant_z((j - 3) // 2)
 
         whiten(NPAIR - 1, 0)
         whiten(NPAIR - 1, 1)
-        finish_z(LAST)
-        for m in range(6, NM):
+        interleave(LAST, 0, 320, "v")
+        interleave(LAST, 320, B, "s")
+        for m in range(NM):
             backproject(m, 2)
         quant_z(LAST, 0, 256)
         quant_z(LAST, 256, B)

import concourse.mybir as mybir
from concourse.masks import make_identity
from contextlib import ExitStack

F32 = mybir.dt.float32
BF16 = mybir.dt.bfloat16
U32 = mybir.dt.uint32
I32 = mybir.dt.int32
U8 = mybir.dt.uint8
FP8 = mybir.dt.float8_e4m3fn
E4M3X4 = mybir.dt.float8_e4m3fn_x4
E2M1X4 = mybir.dt.float4_e2m1fn_x4
ALU = mybir.AluOpType
COPY = mybir.ActivationFunctionType.Copy

D, P, B = 2048, 1024, 512
FLOPS = 2 * 2 * D * P * B

NP = 128
NG = D // 512
NPAIR = 2 * NG
NC = P // 512
NM = P // 128
S_UNITS = []
WARM0 = 6
WARM1 = 1
WC0 = 0
WC1 = 1
SPLIT = 1


def tile_coded_aperture_backprojection_s13_kernel(
    tc, mask_bytes, mask_scale, scenes, dark, inv_sigma, dec_words, dec_scales, out
):
    nc = tc.nc
    with ExitStack() as ctx, tc.manual_schedule():
        keep = ctx.enter_context(tc.tile_pool(name="keep", bufs=1))
        work = ctx.enter_context(tc.tile_pool(name="work", bufs=2))
        psum = ctx.enter_context(tc.psum_pool(name="psum", bufs=1))

        zeros = keep.tile([NP, 512], BF16, name="zeros")
        nc.vector.memset(zeros[:], 0.0)
        mscale = keep.tile([NP, NC, 2, 2], F32, name="mscale")
        nc.scalar.dma_start(
            out=mscale[:], in_=mask_scale.rearrange("o (c p u e) -> p (o c) u e", c=NC, p=NP, u=2, e=2)
        )
        first = keep.tile([NP, 2], BF16, name="first")
        nc.scalar.copy(out=first[:], in_=zeros[:, 0:2])
        darks = keep.tile([NP, NG, 4], BF16, name="darks")
        nc.scalar.dma_start(out=darks[:], in_=dark.rearrange("(g p t) -> p g t", g=NG, p=NP, t=4))
        ident = keep.tile([NP, NP], F32, name="ident")
        make_identity(nc, ident[:])
        gsc = keep.tile([NP, NG, P], U8, name="gsc", align_bytes=64)
        nc.gpsimd.memset(gsc[:].bitcast(I32), 0)

        mask_v = mask_bytes.rearrange("(g p t) k -> g p t k", g=NG, p=NP, t=4)
        sig_v = inv_sigma.rearrange("(g p t) b -> g p t b", g=NG, p=NP, t=4)
        scn_v = scenes.rearrange("(r p) k -> r p k", p=NP)

        mb = [keep.tile([NP, 2, P], U8, name=f"mb{j}", align_bytes=64) for j in range(NPAIR)]
        sig = [keep.tile([NP, 4, B], BF16, name=f"sig{g}", align_bytes=64) for g in range(NG)]
        scn = [keep.tile([NP, P], BF16, name=f"scn{r}", align_bytes=64) for r in range(4)]
        gw = [keep.tile([NP, 2 * P], U8, name=f"gw{g}", align_bytes=64) for g in range(NG)]

        def load_mask(j):
            g, h = divmod(j, 2)
            nc.sync.dma_start(out=mb[j][:], in_=mask_v[g][:, 2 * h : 2 * h + 2, :])

        for j in range(2):
            for t in range(2):
                nc.sync.dma_start(out=mb[j][:, t, :], in_=mask_v[0][:, 2 * j + t, :])
        for r in range(2):
            nc.sync.dma_start(out=scn[r][:], in_=scn_v[r])
        load_mask(2)
        for r in range(2, 4):
            nc.sync.dma_start(out=scn[r][:], in_=scn_v[r])
        load_mask(3)
        nc.sync.dma_start(out=sig[0][:], in_=sig_v[0])
        for j in range(4, 8):
            load_mask(j)
            if j % 2 == 1:
                nc.sync.dma_start(out=sig[j // 2 - 1][:], in_=sig_v[j // 2 - 1])
        nc.sync.dma_start(out=sig[3][:], in_=sig_v[3])
        for q in range(4):
            nc.sync.dma_start(
                out=gsc[32 * q : 32 * q + 4].bitcast(I32),
                in_=dec_scales[:, 4 * q : 4 * q + 4, :].bitcast(I32).rearrange("g q n -> q g n"),
            )
        for g in range(NG):
            nc.sync.dma_start(out=gw[g][:].bitcast(I32), in_=dec_words[g].bitcast(I32))

        scodes = keep.tile([NP, NC, B], U32, name="scodes", align_bytes=64)
        sscales = keep.tile([NP, NC, B], U8, name="sscales", align_bytes=64)
        zcodes = [keep.tile([NP, B], U32, name=f"zcodes{g}", align_bytes=64) for g in range(NG)]
        zscales = [keep.tile([NP, B], U8, name=f"zscales{g}", align_bytes=64) for g in range(NG)]
        sq = [keep.tile([NP, B, 4], BF16, name=f"sq{c}", align_bytes=64) for c in range(NC)]

        wide = {}
        tbank = {}
        qin = {}
        codes = {}
        scales = {}
        ybank = {}
        zt = {}
        zq = {}
        img = {}
        part = {}
        pbank = {}
        sbank = {}

        def bank(tag, shape, name):
            t = psum.tile(shape, F32, name=name, tag=tag)
            return t

        def warm(bk, n):
            for i in range(n):
                nc.tensor.matmul(out=bk, lhsT=zeros[:, 0:128], rhs=zeros[:], start=True, stop=True)

        def widen(j, t, c0, c1, engine):
            if j not in wide:
                wide[j] = work.tile([NP, 2, P], BF16, name=f"wide{j}", tag="wide", bufs=4, align_bytes=64)
            src = mb[j][:, t, c0:c1].bitcast(FP8)
            if engine == "v":
                nc.vector.tensor_copy(out=wide[j][:, t, c0:c1], in_=src)
            else:
                nc.scalar.copy(out=wide[j][:, t, c0:c1], in_=src)

        def widen_pair(j):
            wide[j] = work.tile([NP, 2, P], BF16, name=f"wide{j}", tag="wide", bufs=4, align_bytes=64)
            nc.scalar.copy(
                out=wide[j][:].rearrange("p t k -> p (t k)"), in_=mb[j][:].rearrange("p t k -> p (t k)").bitcast(FP8)
            )

        def turn(bk, tiles, c):
            for t in range(2):
                for u in range(2):
                    nc.tensor.transpose(
                        bk[:, u, 128 * t : 128 * t + 128], tiles[t][:, 256 * c + u : 256 * (c + 1) : 2], ident[:]
                    )

        def turn_mask(j, c, n=0):
            w = wide[j][:].bitcast(F32)
            bk = bank(f"t{c}", [NP, 2, 256], f"tb{j}_{c}")
            tbank[j, c] = bk
            warm(bk[:].rearrange("p u x -> p (u x)"), n)
            turn(bk, [w[:, 0, :], w[:, 1, :]], c)

        def turn_scenes(h, c, n=0):
            bk = bank(f"m{2 * h + c}", [NP, 2, 256], f"sb{h}_{c}")
            sbank[h, c] = bk
            warm(bk[:].rearrange("p u x -> p (u x)"), n)
            turn(bk, [scn[2 * h][:].bitcast(F32), scn[2 * h + 1][:].bitcast(F32)], c)

        def empty_scenes(h, c):
            dst = sq[c][:, 256 * h : 256 * (h + 1), :].rearrange("p x t -> p (x t)").bitcast(F32)
            nc.scalar.copy(
                out=dst.rearrange("p (x u) -> p x u", u=2), in_=sbank[h, c][:].rearrange("p u x -> p x u")
            )

        def quant_scenes(c):
            nc.vector.quantize_mx(
                out=scodes[:, c, :].bitcast(E4M3X4),
                scales=sscales[:, c, :],
                in_=sq[c][:].rearrange("p x t -> p (x t)"),
            )

        def product(j, c):
            if j not in qin:
                qin[j] = work.tile([NP, NC, 256, 4], BF16, name=f"qin{j}", tag="qin", bufs=3, align_bytes=64)
            src = tbank[j, c][:].bitcast(BF16).rearrange("p u (x e) -> p x u e", e=2)
            if (j, c) in S_UNITS:
                scale_mask_scalar(src, j, c)
                return
            nc.vector.tensor_tensor(
                out=qin[j][:, c].rearrange("p x (u e) -> p x u e", u=2),
                in0=src,
                in1=mscale[:, c : c + 1].to_broadcast([NP, 256, 2, 2]),
                op=ALU.mult,
            )

        def scale_mask_scalar(src, j, c):
            for u in range(2):
                for e in range(2):
                    nc.scalar.activation(
                        out=qin[j][:, c, :, 2 * u + e],
                        in_=src[:, :, u, e],
                        func=COPY,
                        scale=mscale[:, c, u, e : e + 1],
                    )

        def quant_mask(j):
            codes[j] = work.tile([NP, NC, 256], U32, name=f"codes{j}", tag="codes", bufs=4, align_bytes=64)
            scales[j] = work.tile([NP, NC, 256], U8, name=f"scales{j}", tag="scales", bufs=4, align_bytes=64)
            nc.vector.quantize_mx(
                out=codes[j][:].rearrange("p c x -> p (c x)").bitcast(E4M3X4),
                scales=scales[j][:].rearrange("p c x -> p (c x)"),
                in_=qin[j][:].rearrange("p c x t -> p (c x t)"),
            )

        def project(j, t):
            ybank[j, t] = bank(f"y{t}", [NP, B], f"y{j}_{t}")
            cols = slice(128 * t, 128 * t + 128)
            for c in range(NC):
                nc.tensor.matmul_mx(
                    out=ybank[j, t][:],
                    lhsT=codes[j][:, c, cols].bitcast(E4M3X4),
                    lhsT_scale=scales[j][:, c, cols],
                    rhs=scodes[:, c, :].bitcast(E4M3X4),
                    rhs_scale=sscales[:, c, :],
                    start=(c == 0),
                    stop=(c == NC - 1),
                )

        def whiten(j, t):
            g, h = divmod(j, 2)
            s = 2 * h + t
            if g not in zt:
                zt[g] = work.tile([NP, 4, B], BF16, name=f"zt{g}", tag="zt", bufs=2, align_bytes=64)
            nc.vector.scalar_tensor_tensor(
                out=zt[g][:, s, :],
                in0=ybank[j, t][:],
                scalar=darks[:, g, s : s + 1],
                in1=sig[g][:, s, :],
                op0=ALU.subtract,
                op1=ALU.mult,
            )

        def interleave(g, b0, b1, engine):
            if g not in zq:
                zq[g] = work.tile([NP, B, 4], BF16, name=f"zq{g}", tag="zq", bufs=2, align_bytes=64)
            dst = zq[g][:, b0:b1, :].rearrange("p (c i) t -> p c t i", i=4)
            src = zt[g][:, :, b0:b1].rearrange("p t (c i) -> p c t i", i=4)
            if engine == "v":
                nc.vector.tensor_copy(out=dst, in_=src)
            else:
                nc.scalar.copy(out=dst, in_=src)

        def quant_z(g, b0=0, b1=B):
            nc.vector.quantize_mx(
                out=zcodes[g][:, b0:b1].bitcast(E4M3X4),
                scales=zscales[g][:, b0:b1],
                in_=zq[g][:, b0:b1, :].rearrange("p b t -> p (b t)"),
            )

        IMG_TAG = ["m0", "m1", "m2", "m3", "t0", "t1", "y0", "y1"]
        LAST = NG - 1

        def image_pass(bk, m, g, start, stop):
            nc.tensor.matmul_mx(
                out=bk[:],
                lhsT=gw[g][:, 256 * m : 256 * (m + 1)].bitcast(E2M1X4),
                lhsT_scale=gsc[:, g, 128 * m : 128 * (m + 1)],
                rhs=zcodes[g][:].bitcast(E4M3X4),
                rhs_scale=zscales[g][:],
                start=start,
                stop=stop,
            )

        def early(m, g):
            if g == 0:
                pbank[m] = bank(f"m{m - 4}", [NP, B], f"early{m}")
            image_pass(pbank[m], m, g, g == 0, g == 1)

        def park(m):
            part[m] = keep.tile([NP, B], F32, name=f"part{m}")
            nc.scalar.copy(out=part[m][:], in_=pbank[m][:])

        def backproject(m, g):
            g0 = 0 if m < 4 else 2
            if g == g0:
                img[m] = bank(IMG_TAG[m], [NP, B], f"img{m}")
            image_pass(img[m], m, g, g == g0, g == LAST)

        wb = bank("y0", [NP, B], "warmbank")
        warm(wb[:], WARM0)
        widen(0, 0, 0, 512, "v")
        widen(0, 1, 0, 512, "s")
        widen(0, 0, 512, P, "v")
        widen(0, 1, 512, P, "v")
        widen(1, 0, 0, 512, "v")
        widen(1, 0, 512, P, "s")
        widen(1, 1, 0, P, "s")
        turn_mask(0, 0)
        turn_mask(0, 1)
        product(0, 0)
        turn_scenes(0, 0, WARM1)
        turn_scenes(0, 1)
        turn_mask(1, 0, WARM1)
        product(0, 1)
        turn_mask(1, 1)
        quant_mask(0)
        empty_scenes(0, 0)
        empty_scenes(0, 1)
        widen_pair(2)
        turn_scenes(1, 0, WARM1)
        turn_scenes(1, 1)
        empty_scenes(1, 0)
        empty_scenes(1, 1)
        product(1, 0)
        turn_mask(2, 0, WARM1)
        product(1, 1)
        turn_mask(2, 1)
        quant_scenes(0)
        quant_scenes(1)
        widen_pair(3)
        quant_mask(1)
        project(0, 0)
        project(0, 1)

        for j in range(2, NPAIR):
            if j == 6:
                for m in range(4, NM):
                    early(m, 1)
            product(j, 0)
            if j == 2:
                whiten(0, 0)
                project(1, 0)
            if j + 1 < NPAIR:
                turn_mask(j + 1, 0, WC0)
            product(j, 1)
            if j == 2:
                whiten(0, 1)
            if j == 2 or SPLIT:
                project(j - 1, 1)
            if j == 4:
                early(4, 0)
                early(5, 0)
            if j + 1 < NPAIR:
                turn_mask(j + 1, 1, WC1)
            if j + 2 < NPAIR:
                widen_pair(j + 2)
            if j == 6:
                for m in range(4, NM):
                    park(m)
            whiten(j - 1, 0)
            quant_mask(j)
            whiten(j - 1, 1)
            if j == 4:
                early(6, 0)
                early(7, 0)
            if j == NPAIR - 1:
                for m in range(2):
                    backproject(m, 0)
                    backproject(m, 1)
            project(j, 0)
            if not SPLIT or j == NPAIR - 1:
                project(j, 1)
            if j == 6:
                for m in range(2, 4):
                    backproject(m, 0)
                    backproject(m, 1)
            if j % 2 == 0:
                g = j // 2 - 1
                interleave(g, 0, 256, "s")
                interleave(g, 256, B, "s")
            else:
                quant_z((j - 3) // 2)

        whiten(NPAIR - 1, 0)
        whiten(NPAIR - 1, 1)
        interleave(LAST, 0, 320, "v")
        interleave(LAST, 320, B, "s")
        for m in range(NM):
            backproject(m, 2)
        quant_z(LAST, 0, 256)
        quant_z(LAST, 256, B)
        out_v = out.rearrange("(m p) b -> m p b", p=NP)
        for m in (0, 4, 1, 5, 2, 6, 3, 7):
            backproject(m, LAST)
            res = work.tile([NP, B], F32, name=f"res{m}", tag="res", bufs=8)
            if m < 4:
                nc.scalar.copy(out=res[:], in_=img[m][:])
            else:
                nc.vector.tensor_tensor(out=res[:], in0=img[m][:], in1=part[m][:], op=ALU.add)
            nc.sync.dma_start(out=out_v[m], in_=res[:])
